import numpy as np
import ml_dtypes


def mxq(x, axis, fmt="e4m3"):
    dtype, down = {"e4m3": (ml_dtypes.float8_e4m3fn, 7), "e5m2": (ml_dtypes.float8_e5m2, 14)}[fmt]
    v = np.moveaxis(np.asarray(x, np.float32).astype(ml_dtypes.bfloat16).astype(np.float64), axis, -1)
    blocks = v.reshape(v.shape[:-1] + (-1, 32))
    amax = np.abs(blocks).max(-1, keepdims=True)
    byte = np.maximum(np.where(amax > 0, np.frexp(amax)[1] - 1 + 127, 0) - down, 1)
    scale = np.exp2(byte - 127.0)
    codes = (blocks / scale).astype(np.float32).astype(dtype).astype(np.float64)
    return np.moveaxis((codes * scale).reshape(v.shape), -1, axis)


WIDE = False


def mx_kscale(k):
    if not WIDE:
        return np.ones(k)
    levels = np.array([30, -30])
    if k % 512:
        return np.exp2(np.random.permutation(np.resize(levels, k // 32))).repeat(32)
    a = np.empty((k // 512, 16))
    for p in range(k // 512):
        a[p, :8] = np.random.permutation(np.resize(levels, 8))
        for g in range(8):
            far = levels[np.abs(levels - a[p, g]) >= 10]
            a[p, g + 8] = far[np.random.randint(len(far))]
    return np.exp2(a.ravel()).repeat(32)


def f64(x):
    return np.asarray(x).astype(np.float64)


def planes(y):
    n, m = y.shape
    v = y.astype(np.float32).astype(ml_dtypes.bfloat16).astype(np.float64).reshape(n // 32, 32, m)
    top = np.abs(v).max(1)
    byte = np.clip(np.where(top > 0, np.frexp(top)[1] - 1 + 127 - 7, 1), 1, 254)
    codes = (v * np.exp2(127.0 - byte)[:, None, :]).reshape(n, m).astype(np.float32).astype(ml_dtypes.float8_e4m3fn).view(np.uint8)
    words = codes.reshape(n // 512, 128, 4, m).transpose(0, 1, 3, 2)
    return np.ascontiguousarray(words), np.ascontiguousarray(byte.astype(np.uint8).reshape(n // 512, 16, m))


K, L, M, T = 1024, 512, 1024, 512


def setup_inputs():
    n = np.random.standard_normal
    s1 = mx_kscale(K)[:, None]
    s2 = mx_kscale(L)[:, None]
    m = np.exp(0.5 * n((1, T)))
    return {
        "w": (n((K, M)) / np.sqrt(K) / s1).astype(np.float32),
        "dy": (m * n((K, T)) * s1).astype(np.float32),
        "v": (n((L, M)) / np.sqrt(L) / s2).astype(np.float32),
        "e": (n((L, T)) * s2).astype(np.float32),
        "r": (n((512, 1024))).astype(np.float32),
    }


def reference(w, dy, v, e, r):
    w_ = mxq(f64(w), 0, "e4m3")
    dy_ = mxq(f64(dy), 0, "e5m2")
    v_ = mxq(f64(v), 0, "e4m3")
    e_ = mxq(f64(e), 0, "e4m3")
    y = dy_.T @ w_ + e_.T @ v_
    out_0 = f64(r) + y
    return (out_0,) + planes(out_0)

@@ -1,0 +1,168 @@
+from contextlib import ExitStack
+
+import concourse.mybir as mybir
+
+K, L, M, T = 1024, 512, 1024, 512
+FLOPS = 2 * (K + L) * M * T
+
+F32 = mybir.dt.float32
+BF16 = mybir.dt.bfloat16
+U32 = mybir.dt.uint32
+I32 = mybir.dt.int32
+U8 = mybir.dt.uint8
+E4M3 = mybir.dt.float8_e4m3fn_x4
+E5M2 = mybir.dt.float8_e5m2_x4
+
+P = 128
+PACK = 4
+K_PASS = P * PACK
+HALF = 512
+LINE = 4
+
+
+def tile_mix_aux_tm_pl_res_kernel(tc, w, dy, v, e, r, out_0, out_1, out_2):
+    nc = tc.nc
+    with ExitStack() as ctx:
+        sb = ctx.enter_context(tc.tile_pool(name="sb", bufs=1))
+        ps = ctx.enter_context(tc.psum_pool(name="ps", bufs=1))
+        ctx.enter_context(tc.manual_schedule())
+
+        def copy_on(engine, out, in_):
+            if engine == "scalar":
+                nc.scalar.copy(out=out, in_=in_)
+            else:
+                nc.vector.tensor_copy(out=out, in_=in_)
+
+        def load(name, rows):
+            raw = sb.tile([P, PACK, rows.shape[1]], F32, name=name)
+            nc.sync.dma_start(out=raw[:], in_=rows.rearrange("(p j) c -> p j c", j=PACK))
+            return raw
+
+        def interleave(engine, grouped, raw):
+            copy_on(
+                engine,
+                grouped.rearrange("p (c n) j -> p c j n", n=LINE),
+                raw.rearrange("p j (c n) -> p c j n", n=LINE),
+            )
+
+        def deal(engine, grouped, raw):
+            copy_on(
+                engine,
+                grouped.rearrange("p (i m) j -> p i m j", i=PACK),
+                raw.rearrange("p j (m i) -> p i m j", i=PACK),
+            )
+
+        def quantize(codes, scales, grouped, fmt):
+            nc.vector.quantize_mx(
+                out=codes.bitcast(fmt), scales=scales, in_=grouped.rearrange("p c j -> p (c j)")
+            )
+
+        def operand(name):
+            grouped = sb.tile([P, HALF, PACK], BF16, name=name + "_bf", align_bytes=64)
+            codes = sb.tile([P, HALF], U32, name=name + "_codes", align_bytes=64)
+            scales = sb.tile([P, HALF], U8, name=name + "_scales", align_bytes=64)
+            return grouped, codes, scales
+
+        token_fmt = [E5M2, E5M2, E4M3]
+        tok = [operand("tok%d" % g) for g in range(3)]
+        wgt = [[operand("wgt%d_%d" % (g, h)) for h in range(2)] for g in range(3)]
+        acc = [[ps.tile([P, HALF], F32, name="acc%d_%d" % (h, i)) for i in range(PACK)] for h in range(2)]
+        res = [sb.tile([P, PACK, HALF], F32, name="res%d" % h) for h in range(2)]
+        res_bf = [sb.tile([P, HALF, PACK], BF16, name="res_bf%d" % h, align_bytes=64) for h in range(2)]
+        res_codes = sb.tile([P, M], U32, name="res_codes", align_bytes=64)
+        res_scales = sb.tile([P, M], U8, name="res_scales", align_bytes=64)
+
+        def cols(h):
+            return slice(h * HALF, (h + 1) * HALF)
+
+        dy_raw0 = load("dy_raw0", dy[0:K_PASS, :])
+        w_raw0 = load("w_raw0", w[0:K_PASS, :])
+        dy_raw1 = load("dy_raw1", dy[K_PASS:K, :])
+        w_raw1 = load("w_raw1", w[K_PASS:K, :])
+        e_raw = load("e_raw", e)
+        v_raw = [load("v_raw%d" % h, v[:, cols(h)]) for h in range(2)]
+        r_rows = r.rearrange("(p i) d -> p i d", i=PACK)
+        out_rows = out_0.rearrange("(p i) d -> p i d", i=PACK)
+        r_sb = [sb.tile([P, PACK, HALF], F32, name="r_sb%d" % h) for h in range(2)]
+        for h in range(2):
+            for i0 in (0, 2):
+                nc.sync.dma_start(out=r_sb[h][:, i0 : i0 + 2, :], in_=r_rows[:, i0 : i0 + 2, cols(h)])
+
+        def quantize_tok(g):
+            quantize(tok[g][1][:], tok[g][2][:], tok[g][0][:], token_fmt[g])
+
+        def quantize_wgt(g, h):
+            quantize(wgt[g][h][1][:], wgt[g][h][2][:], wgt[g][h][0][:], E4M3)
+
+        def multiply(g, h):
+            for i in range(PACK):
+                m_cols = slice(i * P, (i + 1) * P)
+                nc.tensor.matmul_mx(
+                    out=acc[h][i][:],
+                    lhsT=tok[g][1][:, m_cols].bitcast(token_fmt[g]),
+                    lhsT_scale=tok[g][2][:, m_cols],
+                    rhs=wgt[g][h][1][:].bitcast(E4M3),
+                    rhs_scale=wgt[g][h][2][:],
+                    start=(g == 0),
+                    stop=(g == 2),
+                )
+
+        def add(h, i):
+            nc.vector.tensor_tensor(
+                out=res[h][:, i, :], in0=acc[h][i][:], in1=r_sb[h][:, i, :], op=mybir.AluOpType.add
+            )
+
+        def store_rows(h, i0):
+            nc.sync.dma_start(out=out_rows[:, i0 : i0 + 2, cols(h)], in_=res[h][:, i0 : i0 + 2, :])
+
+        def quantize_res(h):
+            quantize(res_codes[:, cols(h)], res_scales[:, cols(h)], res_bf[h][:], E4M3)
+
+        words = out_1[0].rearrange("p d i -> p (d i)").bitcast(I32)
+
+        def store_words(h):
+            nc.sync.dma_start(out=words[:, cols(h)], in_=res_codes[:, cols(h)].bitcast(I32))
+
+        for g, (t_raw, w_raw) in enumerate(((dy_raw0, w_raw0), (dy_raw1, w_raw1))):
+            deal("scalar", tok[g][0][:], t_raw[:])
+            quantize_tok(g)
+            interleave("scalar", wgt[g][1][0][:], w_raw[:, :, cols(1)])
+            interleave("vector", wgt[g][0][0][:], w_raw[:, :, cols(0)])
+            quantize_wgt(g, 0)
+            multiply(g, 0)
+            if g == 1:
+                deal("vector", tok[2][0][:], e_raw[:])
+            quantize_wgt(g, 1)
+            multiply(g, 1)
+        quantize_tok(2)
+        interleave("vector", wgt[2][0][0][:], v_raw[0][:])
+        quantize_wgt(2, 0)
+        multiply(2, 0)
+        interleave("scalar", wgt[2][1][0][:], v_raw[1][:])
+        add(0, 0)
+        add(0, 1)
+        store_rows(0, 0)
+        quantize_wgt(2, 1)
+        multiply(2, 1)
+        add(0, 2)
+        add(0, 3)
+        store_rows(0, 2)
+        interleave("scalar", res_bf[0][:], res[0][:])
+        add(1, 0)
+        add(1, 1)
+        store_rows(1, 0)
+        add(1, 2)
+        add(1, 3)
+        store_rows(1, 2)
+        split = HALF // 2
+        interleave("scalar", res_bf[1][:, split:, :], res[1][:, :, split:])
+        quantize_res(0)
+        store_words(0)
+        interleave("vector", res_bf[1][:, :split, :], res[1][:, :, :split])
+        quantize_res(1)
+        store_words(1)
+        for q in range(4):
+            nc.scalar.dma_start(
+                out=out_2[0, 4 * q : 4 * q + 4, :].bitcast(I32),
+                in_=res_scales[32 * q : 32 * q + 4, :].bitcast(I32),
+            )

@@ -45,12 +45,16 @@ def tile_mix_aux_tm_pl_res_kernel(tc, w, dy, v, e, r, out_0, out_1, out_2):
                 raw.rearrange("p j (c n) -> p c j n", n=LINE),
             )
 
-        def deal(engine, grouped, raw):
+        def deal(engine, grouped, raw, i0=0, i1=PACK):
             copy_on(
                 engine,
-                grouped.rearrange("p (i m) j -> p i m j", i=PACK),
-                raw.rearrange("p j (m i) -> p i m j", i=PACK),
+                grouped.rearrange("p (i m) j -> p i m j", i=PACK)[:, i0:i1],
+                raw.rearrange("p j (m i) -> p i m j", i=PACK)[:, i0:i1],
             )
+
+        def share(grouped, raw, split):
+            interleave("scalar", grouped[:, split:, :], raw[:, :, split:])
+            interleave("vector", grouped[:, :split, :], raw[:, :, :split])
 
         def quantize(codes, scales, grouped, fmt):
             nc.vector.quantize_mx(
@@ -84,9 +88,8 @@ def tile_mix_aux_tm_pl_res_kernel(tc, w, dy, v, e, r, out_0, out_1, out_2):
         r_rows = r.rearrange("(p i) d -> p i d", i=PACK)
         out_rows = out_0.rearrange("(p i) d -> p i d", i=PACK)
         r_sb = [sb.tile([P, PACK, HALF], F32, name="r_sb%d" % h) for h in range(2)]
-        for h in range(2):
-            for i0 in (0, 2):
-                nc.sync.dma_start(out=r_sb[h][:, i0 : i0 + 2, :], in_=r_rows[:, i0 : i0 + 2, cols(h)])
+        for h, i0, i1 in ((0, 0, 1), (0, 1, 2), (0, 2, 4), (1, 0, 2), (1, 2, 4)):
+            nc.sync.dma_start(out=r_sb[h][:, i0:i1, :], in_=r_rows[:, i0:i1, cols(h)])
 
         def quantize_tok(g):
             quantize(tok[g][1][:], tok[g][2][:], tok[g][0][:], token_fmt[g])
@@ -107,9 +110,9 @@ def tile_mix_aux_tm_pl_res_kernel(tc, w, dy, v, e, r, out_0, out_1, out_2):
                     stop=(g == 2),
                 )
 
-        def add(h, i):
+        def add(h, i, c=slice(0, HALF)):
             nc.vector.tensor_tensor(
-                out=res[h][:, i, :], in0=acc[h][i][:], in1=r_sb[h][:, i, :], op=mybir.AluOpType.add
+                out=res[h][:, i, c], in0=acc[h][i][:, c], in1=r_sb[h][:, i, c], op=mybir.AluOpType.add
             )
 
         def store_rows(h, i0):
@@ -124,26 +127,28 @@ def tile_mix_aux_tm_pl_res_kernel(tc, w, dy, v, e, r, out_0, out_1, out_2):
             nc.sync.dma_start(out=words[:, cols(h)], in_=res_codes[:, cols(h)].bitcast(I32))
 
         for g, (t_raw, w_raw) in enumerate(((dy_raw0, w_raw0), (dy_raw1, w_raw1))):
-            deal("scalar", tok[g][0][:], t_raw[:])
+            deal("vector", tok[g][0][:], t_raw[:], 0, 2)
+            deal("scalar", tok[g][0][:], t_raw[:], 2, 4)
             quantize_tok(g)
             interleave("scalar", wgt[g][1][0][:], w_raw[:, :, cols(1)])
             interleave("vector", wgt[g][0][0][:], w_raw[:, :, cols(0)])
             quantize_wgt(g, 0)
             multiply(g, 0)
             if g == 1:
-                deal("vector", tok[2][0][:], e_raw[:])
+                deal("vector", tok[2][0][:], e_raw[:], 0, 2)
+                deal("scalar", tok[2][0][:], e_raw[:], 2, 4)
             quantize_wgt(g, 1)
             multiply(g, 1)
         quantize_tok(2)
-        interleave("vector", wgt[2][0][0][:], v_raw[0][:])
+        share(wgt[2][0][0], v_raw[0], 336)
         quantize_wgt(2, 0)
         multiply(2, 0)
-        interleave("scalar", wgt[2][1][0][:], v_raw[1][:])
+        share(wgt[2][1][0], v_raw[1], 256)
         add(0, 0)
-        add(0, 1)
-        store_rows(0, 0)
         quantize_wgt(2, 1)
         multiply(2, 1)
+        add(0, 1)
+        store_rows(0, 0)
         add(0, 2)
         add(0, 3)
         store_rows(0, 2)
@@ -151,18 +156,19 @@ def tile_mix_aux_tm_pl_res_kernel(tc, w, dy, v, e, r, out_0, out_1, out_2):
         add(1, 0)
         add(1, 1)
         store_rows(1, 0)
+        split = 256
         add(1, 2)
-        add(1, 3)
+        add(1, 3, slice(0, split))
+        add(1, 3, slice(split, HALF))
         store_rows(1, 2)
-        split = HALF // 2
-        interleave("scalar", res_bf[1][:, split:, :], res[1][:, :, split:])
+        share(res_bf[1], res[1], split)
         quantize_res(0)
         store_words(0)
-        interleave("vector", res_bf[1][:, :split, :], res[1][:, :, :split])
         quantize_res(1)
         store_words(1)
         for q in range(4):
-            nc.scalar.dma_start(
+            queue = nc.scalar if q < 2 else nc.sync
+            queue.dma_start(
                 out=out_2[0, 4 * q : 4 * q + 4, :].bitcast(I32),
                 in_=res_scales[32 * q : 32 * q + 4, :].bitcast(I32),
             )

@@ -45,11 +45,11 @@ def tile_mix_aux_tm_pl_res_kernel(tc, w, dy, v, e, r, out_0, out_1, out_2):
                 raw.rearrange("p j (c n) -> p c j n", n=LINE),
             )
 
-        def deal(engine, grouped, raw, i0=0, i1=PACK):
+        def deal(engine, grouped, raw, m0, m1):
             copy_on(
                 engine,
-                grouped.rearrange("p (i m) j -> p i m j", i=PACK)[:, i0:i1],
-                raw.rearrange("p j (m i) -> p i m j", i=PACK)[:, i0:i1],
+                grouped.rearrange("p (i m) j -> p m i j", i=PACK)[:, m0:m1],
+                raw.rearrange("p j (m i) -> p m i j", i=PACK)[:, m0:m1],
             )
 
         def share(grouped, raw, split):
@@ -88,7 +88,7 @@ def tile_mix_aux_tm_pl_res_kernel(tc, w, dy, v, e, r, out_0, out_1, out_2):
         r_rows = r.rearrange("(p i) d -> p i d", i=PACK)
         out_rows = out_0.rearrange("(p i) d -> p i d", i=PACK)
         r_sb = [sb.tile([P, PACK, HALF], F32, name="r_sb%d" % h) for h in range(2)]
-        for h, i0, i1 in ((0, 0, 1), (0, 1, 2), (0, 2, 4), (1, 0, 2), (1, 2, 4)):
+        for h, i0, i1 in ((0, 0, 1), (0, 1, 2), (0, 2, 4), (1, 0, 2), (1, 2, 3), (1, 3, 4)):
             nc.sync.dma_start(out=r_sb[h][:, i0:i1, :], in_=r_rows[:, i0:i1, cols(h)])
 
         def quantize_tok(g):
@@ -118,37 +118,39 @@ def tile_mix_aux_tm_pl_res_kernel(tc, w, dy, v, e, r, out_0, out_1, out_2):
         def store_rows(h, i0):
             nc.sync.dma_start(out=out_rows[:, i0 : i0 + 2, cols(h)], in_=res[h][:, i0 : i0 + 2, :])
 
-        def quantize_res(h):
-            quantize(res_codes[:, cols(h)], res_scales[:, cols(h)], res_bf[h][:], E4M3)
+        def quantize_res(h, c0=0, c1=HALF):
+            c = slice(h * HALF + c0, h * HALF + c1)
+            quantize(res_codes[:, c], res_scales[:, c], res_bf[h][:, c0:c1, :], E4M3)
 
         words = out_1[0].rearrange("p d i -> p (d i)").bitcast(I32)
 
-        def store_words(h):
-            nc.sync.dma_start(out=words[:, cols(h)], in_=res_codes[:, cols(h)].bitcast(I32))
+        def store_words(h, c0=0, c1=HALF):
+            c = slice(h * HALF + c0, h * HALF + c1)
+            nc.sync.dma_start(out=words[:, c], in_=res_codes[:, c].bitcast(I32))
 
         for g, (t_raw, w_raw) in enumerate(((dy_raw0, w_raw0), (dy_raw1, w_raw1))):
-            deal("vector", tok[g][0][:], t_raw[:], 0, 2)
-            deal("scalar", tok[g][0][:], t_raw[:], 2, 4)
+            deal("vector", tok[g][0][:], t_raw[:], 0, 80)
+            deal("scalar", tok[g][0][:], t_raw[:], 80, P)
             quantize_tok(g)
             interleave("scalar", wgt[g][1][0][:], w_raw[:, :, cols(1)])
             interleave("vector", wgt[g][0][0][:], w_raw[:, :, cols(0)])
             quantize_wgt(g, 0)
             multiply(g, 0)
             if g == 1:
-                deal("vector", tok[2][0][:], e_raw[:], 0, 2)
-                deal("scalar", tok[2][0][:], e_raw[:], 2, 4)
+                deal("vector", tok[2][0][:], e_raw[:], 0, 80)
+                deal("scalar", tok[2][0][:], e_raw[:], 80, P)
             quantize_wgt(g, 1)
             multiply(g, 1)
         quantize_tok(2)
         share(wgt[2][0][0], v_raw[0], 336)
         quantize_wgt(2, 0)
         multiply(2, 0)
-        share(wgt[2][1][0], v_raw[1], 256)
+        share(wgt[2][1][0], v_raw[1], 224)
         add(0, 0)
-        quantize_wgt(2, 1)
-        multiply(2, 1)
         add(0, 1)
         store_rows(0, 0)
+        quantize_wgt(2, 1)
+        multiply(2, 1)
         add(0, 2)
         add(0, 3)
         store_rows(0, 2)
@@ -158,14 +160,17 @@ def tile_mix_aux_tm_pl_res_kernel(tc, w, dy, v, e, r, out_0, out_1, out_2):
         store_rows(1, 0)
         split = 256
         add(1, 2)
-        add(1, 3, slice(0, split))
         add(1, 3, slice(split, HALF))
+        interleave("scalar", res_bf[1][:, split:, :], res[1][:, :, split:])
+        add(1, 3, slice(0, split))
         store_rows(1, 2)
-        share(res_bf[1], res[1], split)
         quantize_res(0)
         store_words(0)
-        quantize_res(1)
-        store_words(1)
+        interleave("vector", res_bf[1][:, :split, :], res[1][:, :, :split])
+        quantize_res(1, split, HALF)
+        store_words(1, split, HALF)
+        quantize_res(1, 0, split)
+        store_words(1, 0, split)
         for q in range(4):
             queue = nc.scalar if q < 2 else nc.sync
             queue.dma_start(

@@ -33,9 +33,9 @@ def tile_mix_aux_tm_pl_res_kernel(tc, w, dy, v, e, r, out_0, out_1, out_2):
             else:
                 nc.vector.tensor_copy(out=out, in_=in_)
 
-        def load(name, rows):
+        def load(name, rows, queue=nc.sync):
             raw = sb.tile([P, PACK, rows.shape[1]], F32, name=name)
-            nc.sync.dma_start(out=raw[:], in_=rows.rearrange("(p j) c -> p j c", j=PACK))
+            queue.dma_start(out=raw[:], in_=rows.rearrange("(p j) c -> p j c", j=PACK))
             return raw
 
         def interleave(engine, grouped, raw):
@@ -79,12 +79,13 @@ def tile_mix_aux_tm_pl_res_kernel(tc, w, dy, v, e, r, out_0, out_1, out_2):
         def cols(h):
             return slice(h * HALF, (h + 1) * HALF)
 
+        v_raw0 = load("v_raw0", v[:, cols(0)], nc.scalar)
         dy_raw0 = load("dy_raw0", dy[0:K_PASS, :])
         w_raw0 = load("w_raw0", w[0:K_PASS, :])
         dy_raw1 = load("dy_raw1", dy[K_PASS:K, :])
         w_raw1 = load("w_raw1", w[K_PASS:K, :])
         e_raw = load("e_raw", e)
-        v_raw = [load("v_raw%d" % h, v[:, cols(h)]) for h in range(2)]
+        v_raw = [v_raw0, load("v_raw1", v[:, cols(1)])]
         r_rows = r.rearrange("(p i) d -> p i d", i=PACK)
         out_rows = out_0.rearrange("(p i) d -> p i d", i=PACK)
         r_sb = [sb.tile([P, PACK, HALF], F32, name="r_sb%d" % h) for h in range(2)]
@@ -115,8 +116,8 @@ def tile_mix_aux_tm_pl_res_kernel(tc, w, dy, v, e, r, out_0, out_1, out_2):
                 out=res[h][:, i, c], in0=acc[h][i][:, c], in1=r_sb[h][:, i, c], op=mybir.AluOpType.add
             )
 
-        def store_rows(h, i0):
-            nc.sync.dma_start(out=out_rows[:, i0 : i0 + 2, cols(h)], in_=res[h][:, i0 : i0 + 2, :])
+        def store_rows(h, i0, queue=nc.sync):
+            queue.dma_start(out=out_rows[:, i0 : i0 + 2, cols(h)], in_=res[h][:, i0 : i0 + 2, :])
 
         def quantize_res(h, c0=0, c1=HALF):
             c = slice(h * HALF + c0, h * HALF + c1)
@@ -132,19 +133,22 @@ def tile_mix_aux_tm_pl_res_kernel(tc, w, dy, v, e, r, out_0, out_1, out_2):
             deal("vector", tok[g][0][:], t_raw[:], 0, 80)
             deal("scalar", tok[g][0][:], t_raw[:], 80, P)
             quantize_tok(g)
+            if g == 0:
+                share(wgt[2][0][0], v_raw[0], 336)
+                quantize_wgt(2, 0)
             interleave("scalar", wgt[g][1][0][:], w_raw[:, :, cols(1)])
             interleave("vector", wgt[g][0][0][:], w_raw[:, :, cols(0)])
             quantize_wgt(g, 0)
             multiply(g, 0)
-            if g == 1:
-                deal("vector", tok[2][0][:], e_raw[:], 0, 80)
-                deal("scalar", tok[2][0][:], e_raw[:], 80, P)
-            quantize_wgt(g, 1)
-            multiply(g, 1)
+            if g == 0:
+                quantize_wgt(g, 1)
+                multiply(g, 1)
+        deal("vector", tok[2][0][:], e_raw[:], 0, 80)
+        deal("scalar", tok[2][0][:], e_raw[:], 80, P)
+        quantize_wgt(1, 1)
         quantize_tok(2)
-        share(wgt[2][0][0], v_raw[0], 336)
-        quantize_wgt(2, 0)
         multiply(2, 0)
+        multiply(1, 1)
         share(wgt[2][1][0], v_raw[1], 224)
         add(0, 0)
         add(0, 1)
@@ -153,7 +157,7 @@ def tile_mix_aux_tm_pl_res_kernel(tc, w, dy, v, e, r, out_0, out_1, out_2):
         multiply(2, 1)
         add(0, 2)
         add(0, 3)
-        store_rows(0, 2)
+        store_rows(0, 2, nc.scalar)
         interleave("scalar", res_bf[0][:], res[0][:])
         add(1, 0)
         add(1, 1)

@@ -89,7 +89,7 @@ def tile_mix_aux_tm_pl_res_kernel(tc, w, dy, v, e, r, out_0, out_1, out_2):
         r_rows = r.rearrange("(p i) d -> p i d", i=PACK)
         out_rows = out_0.rearrange("(p i) d -> p i d", i=PACK)
         r_sb = [sb.tile([P, PACK, HALF], F32, name="r_sb%d" % h) for h in range(2)]
-        for h, i0, i1 in ((0, 0, 1), (0, 1, 2), (0, 2, 4), (1, 0, 2), (1, 2, 3), (1, 3, 4)):
+        for h, i0, i1 in ((0, 0, 1), (0, 1, 3), (0, 3, 4), (1, 0, 1), (1, 1, 2), (1, 2, 3), (1, 3, 4)):
             nc.sync.dma_start(out=r_sb[h][:, i0:i1, :], in_=r_rows[:, i0:i1, cols(h)])
 
         def quantize_tok(g):
@@ -116,8 +116,8 @@ def tile_mix_aux_tm_pl_res_kernel(tc, w, dy, v, e, r, out_0, out_1, out_2):
                 out=res[h][:, i, c], in0=acc[h][i][:, c], in1=r_sb[h][:, i, c], op=mybir.AluOpType.add
             )
 
-        def store_rows(h, i0, queue=nc.sync):
-            queue.dma_start(out=out_rows[:, i0 : i0 + 2, cols(h)], in_=res[h][:, i0 : i0 + 2, :])
+        def store_rows(h, i0, queue=nc.sync, n=2):
+            queue.dma_start(out=out_rows[:, i0 : i0 + n, cols(h)], in_=res[h][:, i0 : i0 + n, :])
 
         def quantize_res(h, c0=0, c1=HALF):
             c = slice(h * HALF + c0, h * HALF + c1)
@@ -151,14 +151,26 @@ def tile_mix_aux_tm_pl_res_kernel(tc, w, dy, v, e, r, out_0, out_1, out_2):
         multiply(1, 1)
         share(wgt[2][1][0], v_raw[1], 224)
         add(0, 0)
-        add(0, 1)
-        store_rows(0, 0)
+        store_rows(0, 0, n=1)
+        nc.scalar.copy(out=res[0][:, 2, :], in_=acc[0][2][:])
         quantize_wgt(2, 1)
         multiply(2, 1)
-        add(0, 2)
+        nc.gpsimd.tensor_tensor(
+            out=res[0][:, 2, :], in0=res[0][:, 2, :], in1=r_sb[0][:, 2, :], op=mybir.AluOpType.add
+        )
+        add(0, 1)
+        store_rows(0, 1, n=1)
         add(0, 3)
         store_rows(0, 2, nc.scalar)
-        interleave("scalar", res_bf[0][:], res[0][:])
+        nc.gpsimd.tensor_scalar(
+            out=res_bf[0][:, :192, :],
+            in0=res[0][:, :, :192].rearrange("p i c -> p c i"),
+            scalar1=1.0,
+            scalar2=-0.0,
+            op0=mybir.AluOpType.mult,
+            op1=mybir.AluOpType.add,
+        )
+        interleave("scalar", res_bf[0][:, 192:, :], res[0][:, :, 192:])
         add(1, 0)
         add(1, 1)
         store_rows(1, 0)

@@ -187,9 +187,7 @@ def tile_mix_aux_tm_pl_res_kernel(tc, w, dy, v, e, r, out_0, out_1, out_2):
         store_words(1, split, HALF)
         quantize_res(1, 0, split)
         store_words(1, 0, split)
-        for q in range(4):
-            queue = nc.scalar if q < 2 else nc.sync
-            queue.dma_start(
-                out=out_2[0, 4 * q : 4 * q + 4, :].bitcast(I32),
-                in_=res_scales[32 * q : 32 * q + 4, :].bitcast(I32),
-            )
+        scale_rows = out_2[0].rearrange("(q n) d -> n q d", n=4)
+        for n in range(4):
+            queue = nc.scalar if n < 2 else nc.sync
+            queue.dma_start(out=scale_rows[n].bitcast(I32), in_=res_scales[n:P:32, :].bitcast(I32))

@@ -18,6 +18,7 @@ PACK = 4
 K_PASS = P * PACK
 HALF = 512
 LINE = 4
+ALIGN = 256
 
 
 def tile_mix_aux_tm_pl_res_kernel(tc, w, dy, v, e, r, out_0, out_1, out_2):
@@ -34,7 +35,7 @@ def tile_mix_aux_tm_pl_res_kernel(tc, w, dy, v, e, r, out_0, out_1, out_2):
                 nc.vector.tensor_copy(out=out, in_=in_)
 
         def load(name, rows, queue=nc.sync):
-            raw = sb.tile([P, PACK, rows.shape[1]], F32, name=name)
+            raw = sb.tile([P, PACK, rows.shape[1]], F32, name=name, align_bytes=ALIGN)
             queue.dma_start(out=raw[:], in_=rows.rearrange("(p j) c -> p j c", j=PACK))
             return raw
 
@@ -62,19 +63,19 @@ def tile_mix_aux_tm_pl_res_kernel(tc, w, dy, v, e, r, out_0, out_1, out_2):
             )
 
         def operand(name):
-            grouped = sb.tile([P, HALF, PACK], BF16, name=name + "_bf", align_bytes=64)
-            codes = sb.tile([P, HALF], U32, name=name + "_codes", align_bytes=64)
-            scales = sb.tile([P, HALF], U8, name=name + "_scales", align_bytes=64)
+            grouped = sb.tile([P, HALF, PACK], BF16, name=name + "_bf", align_bytes=ALIGN)
+            codes = sb.tile([P, HALF], U32, name=name + "_codes", align_bytes=ALIGN)
+            scales = sb.tile([P, HALF], U8, name=name + "_scales", align_bytes=ALIGN)
             return grouped, codes, scales
 
         token_fmt = [E5M2, E5M2, E4M3]
         tok = [operand("tok%d" % g) for g in range(3)]
         wgt = [[operand("wgt%d_%d" % (g, h)) for h in range(2)] for g in range(3)]
         acc = [[ps.tile([P, HALF], F32, name="acc%d_%d" % (h, i)) for i in range(PACK)] for h in range(2)]
-        res = [sb.tile([P, PACK, HALF], F32, name="res%d" % h) for h in range(2)]
-        res_bf = [sb.tile([P, HALF, PACK], BF16, name="res_bf%d" % h, align_bytes=64) for h in range(2)]
-        res_codes = sb.tile([P, M], U32, name="res_codes", align_bytes=64)
-        res_scales = sb.tile([P, M], U8, name="res_scales", align_bytes=64)
+        res = [sb.tile([P, PACK, HALF], F32, name="res%d" % h, align_bytes=ALIGN) for h in range(2)]
+        res_bf = [sb.tile([P, HALF, PACK], BF16, name="res_bf%d" % h, align_bytes=ALIGN) for h in range(2)]
+        res_codes = sb.tile([P, M], U32, name="res_codes", align_bytes=ALIGN)
+        res_scales = sb.tile([P, M], U8, name="res_scales", align_bytes=ALIGN)
 
         def cols(h):
             return slice(h * HALF, (h + 1) * HALF)
@@ -88,7 +89,7 @@ def tile_mix_aux_tm_pl_res_kernel(tc, w, dy, v, e, r, out_0, out_1, out_2):
         v_raw = [v_raw0, load("v_raw1", v[:, cols(1)])]
         r_rows = r.rearrange("(p i) d -> p i d", i=PACK)
         out_rows = out_0.rearrange("(p i) d -> p i d", i=PACK)
-        r_sb = [sb.tile([P, PACK, HALF], F32, name="r_sb%d" % h) for h in range(2)]
+        r_sb = [sb.tile([P, PACK, HALF], F32, name="r_sb%d" % h, align_bytes=ALIGN) for h in range(2)]
         for h, i0, i1 in ((0, 0, 1), (0, 1, 3), (0, 3, 4), (1, 0, 1), (1, 1, 2), (1, 2, 3), (1, 3, 4)):
             nc.sync.dma_start(out=r_sb[h][:, i0:i1, :], in_=r_rows[:, i0:i1, cols(h)])
 

@@ -99,8 +99,8 @@ def tile_mix_aux_tm_pl_res_kernel(tc, w, dy, v, e, r, out_0, out_1, out_2):
         def quantize_wgt(g, h):
             quantize(wgt[g][h][1][:], wgt[g][h][2][:], wgt[g][h][0][:], E4M3)
 
-        def multiply(g, h):
-            for i in range(PACK):
+        def multiply(g, h, rows=range(PACK)):
+            for i in rows:
                 m_cols = slice(i * P, (i + 1) * P)
                 nc.tensor.matmul_mx(
                     out=acc[h][i][:],
@@ -148,14 +148,17 @@ def tile_mix_aux_tm_pl_res_kernel(tc, w, dy, v, e, r, out_0, out_1, out_2):
         deal("scalar", tok[2][0][:], e_raw[:], 80, P)
         quantize_wgt(1, 1)
         quantize_tok(2)
-        multiply(2, 0)
-        multiply(1, 1)
-        share(wgt[2][1][0], v_raw[1], 224)
+        multiply(2, 0, (0, 2, 1, 3))
+        multiply(1, 1, (0, 1))
+        share(wgt[2][1][0], v_raw[1], 256)
         add(0, 0)
         store_rows(0, 0, n=1)
         nc.scalar.copy(out=res[0][:, 2, :], in_=acc[0][2][:])
         quantize_wgt(2, 1)
-        multiply(2, 1)
+        multiply(2, 1, (0, 1))
+        for i in (2, 3):
+            multiply(1, 1, (i,))
+            multiply(2, 1, (i,))
         nc.gpsimd.tensor_tensor(
             out=res[0][:, 2, :], in0=res[0][:, 2, :], in1=r_sb[0][:, 2, :], op=mybir.AluOpType.add
         )
@@ -164,14 +167,14 @@ def tile_mix_aux_tm_pl_res_kernel(tc, w, dy, v, e, r, out_0, out_1, out_2):
         add(0, 3)
         store_rows(0, 2, nc.scalar)
         nc.gpsimd.tensor_scalar(
-            out=res_bf[0][:, :192, :],
-            in0=res[0][:, :, :192].rearrange("p i c -> p c i"),
+            out=res_bf[0][:, :256, :],
+            in0=res[0][:, :, :256].rearrange("p i c -> p c i"),
             scalar1=1.0,
             scalar2=-0.0,
             op0=mybir.AluOpType.mult,
             op1=mybir.AluOpType.add,
         )
-        interleave("scalar", res_bf[0][:, 192:, :], res[0][:, :, 192:])
+        interleave("scalar", res_bf[0][:, 256:, :], res[0][:, :, 256:])
         add(1, 0)
         add(1, 1)
         store_rows(1, 0)

from contextlib import ExitStack

import concourse.mybir as mybir

K, L, M, T = 1024, 512, 1024, 512
FLOPS = 2 * (K + L) * M * T

F32 = mybir.dt.float32
BF16 = mybir.dt.bfloat16
U32 = mybir.dt.uint32
I32 = mybir.dt.int32
U8 = mybir.dt.uint8
E4M3 = mybir.dt.float8_e4m3fn_x4
E5M2 = mybir.dt.float8_e5m2_x4

P = 128
PACK = 4
K_PASS = P * PACK
HALF = 512
LINE = 4
ALIGN = 256


def tile_mix_aux_tm_pl_res_kernel(tc, w, dy, v, e, r, out_0, out_1, out_2):
    nc = tc.nc
    with ExitStack() as ctx:
        sb = ctx.enter_context(tc.tile_pool(name="sb", bufs=1))
        ps = ctx.enter_context(tc.psum_pool(name="ps", bufs=1))
        ctx.enter_context(tc.manual_schedule())

        def copy_on(engine, out, in_):
            if engine == "scalar":
                nc.scalar.copy(out=out, in_=in_)
            else:
                nc.vector.tensor_copy(out=out, in_=in_)

        def load(name, rows, queue=nc.sync):
            raw = sb.tile([P, PACK, rows.shape[1]], F32, name=name, align_bytes=ALIGN)
            queue.dma_start(out=raw[:], in_=rows.rearrange("(p j) c -> p j c", j=PACK))
            return raw

        def interleave(engine, grouped, raw):
            copy_on(
                engine,
                grouped.rearrange("p (c n) j -> p c j n", n=LINE),
                raw.rearrange("p j (c n) -> p c j n", n=LINE),
            )

        def deal(engine, grouped, raw, m0, m1):
            copy_on(
                engine,
                grouped.rearrange("p (i m) j -> p m i j", i=PACK)[:, m0:m1],
                raw.rearrange("p j (m i) -> p m i j", i=PACK)[:, m0:m1],
            )

        def share(grouped, raw, split):
            interleave("scalar", grouped[:, split:, :], raw[:, :, split:])
            interleave("vector", grouped[:, :split, :], raw[:, :, :split])

        def quantize(codes, scales, grouped, fmt):
            nc.vector.quantize_mx(
                out=codes.bitcast(fmt), scales=scales, in_=grouped.rearrange("p c j -> p (c j)")
            )

        def operand(name):
            grouped = sb.tile([P, HALF, PACK], BF16, name=name + "_bf", align_bytes=ALIGN)
            codes = sb.tile([P, HALF], U32, name=name + "_codes", align_bytes=ALIGN)
            scales = sb.tile([P, HALF], U8, name=name + "_scales", align_bytes=ALIGN)
            return grouped, codes, scales

        token_fmt = [E5M2, E5M2, E4M3]
        tok = [operand("tok%d" % g) for g in range(3)]
        wgt = [[operand("wgt%d_%d" % (g, h)) for h in range(2)] for g in range(3)]
        acc = [[ps.tile([P, HALF], F32, name="acc%d_%d" % (h, i)) for i in range(PACK)] for h in range(2)]
        res = [sb.tile([P, PACK, HALF], F32, name="res%d" % h, align_bytes=ALIGN) for h in range(2)]
        res_bf = [sb.tile([P, HALF, PACK], BF16, name="res_bf%d" % h, align_bytes=ALIGN) for h in range(2)]
        res_codes = sb.tile([P, M], U32, name="res_codes", align_bytes=ALIGN)
        res_scales = sb.tile([P, M], U8, name="res_scales", align_bytes=ALIGN)

        def cols(h):
            return slice(h * HALF, (h + 1) * HALF)

        v_raw0 = load("v_raw0", v[:, cols(0)], nc.scalar)
        dy_raw0 = load("dy_raw0", dy[0:K_PASS, :])
        w_raw0 = load("w_raw0", w[0:K_PASS, :])
        dy_raw1 = load("dy_raw1", dy[K_PASS:K, :])
        w_raw1 = load("w_raw1", w[K_PASS:K, :])
        e_raw = load("e_raw", e)
        v_raw = [v_raw0, load("v_raw1", v[:, cols(1)])]
        r_rows = r.rearrange("(p i) d -> p i d", i=PACK)
        out_rows = out_0.rearrange("(p i) d -> p i d", i=PACK)
        r_sb = [sb.tile([P, PACK, HALF], F32, name="r_sb%d" % h, align_bytes=ALIGN) for h in range(2)]
        for h, i0, i1 in ((0, 0, 1), (0, 1, 3), (0, 3, 4), (1, 0, 1), (1, 1, 2), (1, 2, 3), (1, 3, 4)):
            nc.sync.dma_start(out=r_sb[h][:, i0:i1, :], in_=r_rows[:, i0:i1, cols(h)])

        def quantize_tok(g):
            quantize(tok[g][1][:], tok[g][2][:], tok[g][0][:], token_fmt[g])

        def quantize_wgt(g, h):
            quantize(wgt[g][h][1][:], wgt[g][h][2][:], wgt[g][h][0][:], E4M3)

        def multiply(g, h, rows=range(PACK)):
            for i in rows:
                m_cols = slice(i * P, (i + 1) * P)
                nc.tensor.matmul_mx(
                    out=acc[h][i][:],
                    lhsT=tok[g][1][:, m_cols].bitcast(token_fmt[g]),
                    lhsT_scale=tok[g][2][:, m_cols],
                    rhs=wgt[g][h][1][:].bitcast(E4M3),
                    rhs_scale=wgt[g][h][2][:],
                    start=(g == 0),
                    stop=(g == 2),
                )

        def add(h, i, c=slice(0, HALF)):
            nc.vector.tensor_tensor(
                out=res[h][:, i, c], in0=acc[h][i][:, c], in1=r_sb[h][:, i, c], op=mybir.AluOpType.add
            )

        def store_rows(h, i0, queue=nc.sync, n=2):
            queue.dma_start(out=out_rows[:, i0 : i0 + n, cols(h)], in_=res[h][:, i0 : i0 + n, :])

        def quantize_res(h, c0=0, c1=HALF):
            c = slice(h * HALF + c0, h * HALF + c1)
            quantize(res_codes[:, c], res_scales[:, c], res_bf[h][:, c0:c1, :], E4M3)

        words = out_1[0].rearrange("p d i -> p (d i)").bitcast(I32)

        def store_words(h, c0=0, c1=HALF):
            c = slice(h * HALF + c0, h * HALF + c1)
            nc.sync.dma_start(out=words[:, c], in_=res_codes[:, c].bitcast(I32))

        for g, (t_raw, w_raw) in enumerate(((dy_raw0, w_raw0), (dy_raw1, w_raw1))):
            deal("vector", tok[g][0][:], t_raw[:], 0, 80)
            deal("scalar", tok[g][0][:], t_raw[:], 80, P)
            quantize_tok(g)
            if g == 0:
                share(wgt[2][0][0], v_raw[0], 336)
                quantize_wgt(2, 0)
            interleave("scalar", wgt[g][1][0][:], w_raw[:, :, cols(1)])
            interleave("vector", wgt[g][0][0][:], w_raw[:, :, cols(0)])
            quantize_wgt(g, 0)
            multiply(g, 0)
            if g == 0:
                quantize_wgt(g, 1)
                multiply(g, 1)
        deal("vector", tok[2][0][:], e_raw[:], 0, 80)
        deal("scalar", tok[2][0][:], e_raw[:], 80, P)
        quantize_wgt(1, 1)
        quantize_tok(2)
        multiply(2, 0, (0, 2, 1, 3))
        multiply(1, 1, (0, 1))
        share(wgt[2][1][0], v_raw[1], 256)
        add(0, 0)
        store_rows(0, 0, n=1)
        nc.scalar.copy(out=res[0][:, 2, :], in_=acc[0][2][:])
        quantize_wgt(2, 1)
        multiply(2, 1, (0, 1))
        for i in (2, 3):
            multiply(1, 1, (i,))
            multiply(2, 1, (i,))
        nc.gpsimd.tensor_tensor(
            out=res[0][:, 2, :], in0=res[0][:, 2, :], in1=r_sb[0][:, 2, :], op=mybir.AluOpType.add
        )
        add(0, 1)
        store_rows(0, 1, n=1)
        add(0, 3)
        store_rows(0, 2, nc.scalar)
        nc.gpsimd.tensor_scalar(
            out=res_bf[0][:, :256, :],
            in0=res[0][:, :, :256].rearrange("p i c -> p c i"),
            scalar1=1.0,
            scalar2=-0.0,
            op0=mybir.AluOpType.mult,
            op1=mybir.AluOpType.add,
        )
        interleave("scalar", res_bf[0][:, 256:, :], res[0][:, :, 256:])
        add(1, 0)
        add(1, 1)
        store_rows(1, 0)
        split = 256
        add(1, 2)
        add(1, 3, slice(split, HALF))
        interleave("scalar", res_bf[1][:, split:, :], res[1][:, :, split:])
        add(1, 3, slice(0, split))
        store_rows(1, 2)
        quantize_res(0)
        store_words(0)
        interleave("vector", res_bf[1][:, :split, :], res[1][:, :, :split])
        quantize_res(1, split, HALF)
        store_words(1, split, HALF)
        quantize_res(1, 0, split)
        store_words(1, 0, split)
        scale_rows = out_2[0].rearrange("(q n) d -> n q d", n=4)
        for n in range(4):
            queue = nc.scalar if n < 2 else nc.sync
            queue.dma_start(out=scale_rows[n].bitcast(I32), in_=res_scales[n:P:32, :].bitcast(I32))
